import numpy as np
import ml_dtypes


def mxq(x, axis, fmt="e4m3"):
    dtype, down = {"e4m3": (ml_dtypes.float8_e4m3fn, 7), "e5m2": (ml_dtypes.float8_e5m2, 14)}[fmt]
    v = np.moveaxis(np.asarray(x, np.float32).astype(ml_dtypes.bfloat16).astype(np.float64), axis, -1)
    blocks = v.reshape(v.shape[:-1] + (-1, 32))
    amax = np.abs(blocks).max(-1, keepdims=True)
    byte = np.maximum(np.where(amax > 0, np.frexp(amax)[1] - 1 + 127, 0) - down, 1)
    scale = np.exp2(byte - 127.0)
    codes = (blocks / scale).astype(np.float32).astype(dtype).astype(np.float64)
    return np.moveaxis((codes * scale).reshape(v.shape), -1, axis)


WIDE = False


def mx_kscale(k, group=512):
    if not WIDE:
        return np.ones(k)
    levels = np.array([18, -18])
    if group != 512:
        return np.exp2(np.random.permutation(np.resize(levels, k // group))).repeat(group)
    if k % 512:
        return np.exp2(np.random.permutation(np.resize(levels, k // 32))).repeat(32)
    a = np.empty((k // 512, 16))
    for p in range(k // 512):
        a[p, :8] = np.random.permutation(np.resize(levels, 8))
        for g in range(8):
            far = levels[np.abs(levels - a[p, g]) >= 10]
            a[p, g + 8] = far[np.random.randint(len(far))]
    return np.exp2(a.ravel()).repeat(32)


def f64(x):
    return np.asarray(x).astype(np.float64)


E2M1 = np.array([0.0, 0.5, 1.0, 1.5, 2.0, 3.0, 4.0, 6.0, -0.0, -0.5, -1.0, -1.5, -2.0, -3.0, -4.0, -6.0])


def pack_group(w):
    k, n = w.shape
    w = f64(np.asarray(w, np.float32).astype(ml_dtypes.bfloat16)).reshape(k // 32, 32, n)
    amax = np.abs(w).max(1)
    mant, ex = np.frexp(amax / 6.0)
    byte = np.clip(np.where(amax > 0, np.where(mant > 0.5, ex, ex - 1) + 127, 1), 1, 254)
    scaled = (w * np.exp2(127.0 - byte)[:, None, :]).reshape(k, n).astype(np.float32)
    c = np.ascontiguousarray(scaled.reshape(k // 4, 4, n).transpose(0, 2, 1)).astype(ml_dtypes.float4_e2m1fn).view(np.uint8) & 0xF
    return np.ascontiguousarray((c[..., 0::2] | (c[..., 1::2] << 4)).reshape(k // 4, 2 * n)), byte.astype(np.uint8)


def unpack_group(words, scales):
    p, n = words.shape[0], scales.shape[1]
    words = np.ascontiguousarray(words).reshape(p, n, 2)
    nib = np.empty((p, n, 4), np.uint8)
    nib[..., 0::2] = words & 0xF
    nib[..., 1::2] = words >> 4
    return E2M1[nib].transpose(0, 2, 1).reshape(4 * p, n) * np.repeat(np.exp2(scales.astype(np.float64) - 127.0), 32, axis=0)


def silu(v):
    return v / (1.0 + np.exp(-v))


G, D, M, N = 4, 128, 256, 1024


def setup_inputs():
    n = np.random.standard_normal
    s = mx_kscale(D, 0)[:, None]
    w_ = [pack_group(w) for w in n((G, D, M)) / np.sqrt(D) / s]
    return {
        "x": (n((G, D, N)) * s).astype(np.float32),
        "w_words": np.stack([w[0] for w in w_]),
        "w_scales": np.stack([w[1] for w in w_]),
        "r": n((G, M, N)).astype(np.float32),
    }


def reference(x, w_words, w_scales, r):
    xq = mxq(f64(x), 1, "e4m3")
    y = np.stack([unpack_group(w_words[g], w_scales[g]) for g in range(G)]).transpose(0, 2, 1) @ xq
    y = silu(y)
    y = y + f64(r)
    return y

@@ -1,0 +1,117 @@
+from contextlib import ExitStack
+
+import concourse.mybir as mybir
+
+G, D, M, N = 4, 128, 256, 1024
+FLOPS = 2 * G * D * M * N
+
+F32 = mybir.dt.float32
+BF16 = mybir.dt.bfloat16
+I32 = mybir.dt.int32
+U32 = mybir.dt.uint32
+U8 = mybir.dt.uint8
+FP8X4 = mybir.dt.float8_e4m3fn_x4
+FP4X4 = mybir.dt.float4_e2m1fn_x4
+SILU = mybir.ActivationFunctionType.Silu
+ADD = mybir.AluOpType.add
+
+P = 128
+PACK = 4
+ROWS = D // PACK
+BLOCKS = D // 32
+PAIR = M // P
+HALF = 512
+RUN = 4
+
+
+def tile_rows_glin_silu_res_kernel(tc, x, w_words, w_scales, r, out):
+    nc = tc.nc
+    with ExitStack() as ctx:
+        keep = ctx.enter_context(tc.tile_pool(name="keep", bufs=1))
+        acts = ctx.enter_context(tc.tile_pool(name="acts", bufs=4))
+        psum = ctx.enter_context(tc.psum_pool(name="psum", bufs=1))
+        ctx.enter_context(tc.manual_schedule())
+
+        x_raw = keep.tile([P, PACK, N], F32)
+        words_raw = keep.tile([P, 2 * M], U8, align_bytes=64)
+        scales_raw = keep.tile([P, M], U8, align_bytes=64)
+        words = keep.tile([P, 2 * M], U8, align_bytes=64)
+        scales = keep.tile([P, M], U8, align_bytes=64)
+        warm = keep.tile([P, 8], F32)
+        res = [keep.tile([P, PAIR * N], F32, name="res%d" % g) for g in range(G)]
+        grouped = [keep.tile([P, HALF, PACK], BF16, name="grouped%d" % h, align_bytes=64) for h in range(2)]
+        codes = [keep.tile([P, HALF], U32, name="codes%d" % h, align_bytes=64) for h in range(2)]
+        planes = [keep.tile([P, HALF], U8, name="planes%d" % h, align_bytes=64) for h in range(2)]
+        banks = [[psum.tile([P, HALF], F32, name="bank%d_%d" % (g, t)) for t in range(PAIR)] for g in range(G)]
+
+        nc.vector.memset(scales_raw[:].bitcast(I32), 0)
+        nc.vector.memset(warm[:], 0.0)
+        nc.scalar.activation(out=warm[:], in_=warm[:], func=SILU)
+
+        x_rows = x.rearrange("g (p j) n -> (g p) j n", j=PACK)
+        nc.sync.dma_start(out=x_raw[:, 0:2, :], in_=x_rows[:, 0:2, :])
+        nc.sync.dma_start(out=words_raw[:].bitcast(I32), in_=w_words.rearrange("g p b -> (g p) b").bitcast(I32))
+        for g in range(G):
+            nc.sync.dma_start(
+                out=scales_raw[ROWS * g : ROWS * g + BLOCKS, :].bitcast(I32), in_=w_scales[g].bitcast(I32)
+            )
+        nc.sync.dma_start(out=x_raw[:, 2:4, :], in_=x_rows[:, 2:4, :])
+        for g in range(G):
+            nc.sync.dma_start(out=res[g][:], in_=r[g].rearrange("(p t) n -> p (t n)", t=PAIR))
+
+        nc.vector.tensor_copy(
+            out=words[:].rearrange("p (t m b) -> p m t b", t=PAIR, b=2),
+            in_=words_raw[:].rearrange("p (m t b) -> p m t b", t=PAIR, b=2),
+        )
+        nc.vector.tensor_copy(
+            out=scales[:].rearrange("p (t m) -> p m t", t=PAIR),
+            in_=scales_raw[:].rearrange("p (m t) -> p m t", t=PAIR),
+        )
+
+        def views(h):
+            cols = slice(h * HALF, (h + 1) * HALF)
+            return (
+                grouped[h][:].rearrange("p (c i) j -> p c j i", i=RUN),
+                x_raw[:, :, cols].rearrange("p j (c i) -> p c j i", i=RUN),
+            )
+
+        def quantize(h):
+            nc.vector.quantize_mx(
+                out=codes[h][:].bitcast(FP8X4),
+                scales=planes[h][:],
+                in_=grouped[h][:].rearrange("p c j -> p (c j)"),
+            )
+
+        dst, src = views(0)
+        nc.vector.tensor_copy(out=dst, in_=src)
+        dst, src = views(1)
+        nc.scalar.copy(out=dst, in_=src)
+        quantize(0)
+        quantize(1)
+
+        def unit(g, t, h):
+            rows = slice(ROWS * g, ROWS * (g + 1))
+            nc.tensor.matmul_mx(
+                out=banks[g][t][:],
+                lhsT=words[rows, 2 * P * t : 2 * P * (t + 1)].bitcast(FP4X4),
+                lhsT_scale=scales[rows, P * t : P * (t + 1)],
+                rhs=codes[h][rows, :].bitcast(FP8X4),
+                rhs_scale=planes[h][rows, :],
+                start=True,
+                stop=True,
+            )
+            act = acts.tile([P, HALF], F32)
+            nc.scalar.activation(out=act[:], in_=banks[g][t][:], func=SILU)
+            cols = slice(t * N + h * HALF, t * N + (h + 1) * HALF)
+            nc.vector.tensor_tensor(out=res[g][:, cols], in0=act[:], in1=res[g][:, cols], op=ADD)
+
+        unit(0, 0, 0)
+        unit(0, 1, 0)
+        for g in range(G):
+            if g + 1 < G:
+                unit(g + 1, 0, 0)
+            unit(g, 0, 1)
+            unit(g, 1, 1)
+            nc.sync.dma_start(out=out[g].rearrange("(p t) n -> p (t n)", t=PAIR), in_=res[g][:])
+            if g + 1 < G:
+                unit(g + 1, 1, 0)

@@ -28,16 +28,15 @@ def tile_rows_glin_silu_res_kernel(tc, x, w_words, w_scales, r, out):
     nc = tc.nc
     with ExitStack() as ctx:
         keep = ctx.enter_context(tc.tile_pool(name="keep", bufs=1))
-        acts = ctx.enter_context(tc.tile_pool(name="acts", bufs=4))
         psum = ctx.enter_context(tc.psum_pool(name="psum", bufs=1))
         ctx.enter_context(tc.manual_schedule())
 
-        x_raw = keep.tile([P, PACK, N], F32)
+        x_raw = [keep.tile([P, PACK, HALF], F32, name="x_raw%d" % h) for h in range(2)]
         words_raw = keep.tile([P, 2 * M], U8, align_bytes=64)
         scales_raw = keep.tile([P, M], U8, align_bytes=64)
         words = keep.tile([P, 2 * M], U8, align_bytes=64)
         scales = keep.tile([P, M], U8, align_bytes=64)
-        warm = keep.tile([P, 8], F32)
+        act = [keep.tile([P, PAIR * N], F32, name="act%d" % g) for g in range(G)]
         res = [keep.tile([P, PAIR * N], F32, name="res%d" % g) for g in range(G)]
         grouped = [keep.tile([P, HALF, PACK], BF16, name="grouped%d" % h, align_bytes=64) for h in range(2)]
         codes = [keep.tile([P, HALF], U32, name="codes%d" % h, align_bytes=64) for h in range(2)]
@@ -45,34 +44,22 @@ def tile_rows_glin_silu_res_kernel(tc, x, w_words, w_scales, r, out):
         banks = [[psum.tile([P, HALF], F32, name="bank%d_%d" % (g, t)) for t in range(PAIR)] for g in range(G)]
 
         nc.vector.memset(scales_raw[:].bitcast(I32), 0)
-        nc.vector.memset(warm[:], 0.0)
-        nc.scalar.activation(out=warm[:], in_=warm[:], func=SILU)
 
         x_rows = x.rearrange("g (p j) n -> (g p) j n", j=PACK)
-        nc.sync.dma_start(out=x_raw[:, 0:2, :], in_=x_rows[:, 0:2, :])
+        nc.sync.dma_start(out=x_raw[0][:], in_=x_rows[:, :, 0:HALF])
         nc.sync.dma_start(out=words_raw[:].bitcast(I32), in_=w_words.rearrange("g p b -> (g p) b").bitcast(I32))
         for g in range(G):
             nc.sync.dma_start(
                 out=scales_raw[ROWS * g : ROWS * g + BLOCKS, :].bitcast(I32), in_=w_scales[g].bitcast(I32)
             )
-        nc.sync.dma_start(out=x_raw[:, 2:4, :], in_=x_rows[:, 2:4, :])
+        nc.sync.dma_start(out=x_raw[1][:], in_=x_rows[:, :, HALF:N])
         for g in range(G):
             nc.sync.dma_start(out=res[g][:], in_=r[g].rearrange("(p t) n -> p (t n)", t=PAIR))
 
-        nc.vector.tensor_copy(
-            out=words[:].rearrange("p (t m b) -> p m t b", t=PAIR, b=2),
-            in_=words_raw[:].rearrange("p (m t b) -> p m t b", t=PAIR, b=2),
-        )
-        nc.vector.tensor_copy(
-            out=scales[:].rearrange("p (t m) -> p m t", t=PAIR),
-            in_=scales_raw[:].rearrange("p (m t) -> p m t", t=PAIR),
-        )
-
-        def views(h):
-            cols = slice(h * HALF, (h + 1) * HALF)
-            return (
-                grouped[h][:].rearrange("p (c i) j -> p c j i", i=RUN),
-                x_raw[:, :, cols].rearrange("p j (c i) -> p c j i", i=RUN),
+        def interleave(h):
+            nc.vector.tensor_copy(
+                out=grouped[h][:].rearrange("p (c i) j -> p c j i", i=RUN),
+                in_=x_raw[h][:].rearrange("p j (c i) -> p c j i", i=RUN),
             )
 
         def quantize(h):
@@ -82,14 +69,20 @@ def tile_rows_glin_silu_res_kernel(tc, x, w_words, w_scales, r, out):
                 in_=grouped[h][:].rearrange("p c j -> p (c j)"),
             )
 
-        dst, src = views(0)
-        nc.vector.tensor_copy(out=dst, in_=src)
-        dst, src = views(1)
-        nc.scalar.copy(out=dst, in_=src)
+        interleave(0)
+        nc.vector.tensor_copy(
+            out=words[:].rearrange("p (t m b) -> p m t b", t=PAIR, b=2),
+            in_=words_raw[:].rearrange("p (m t b) -> p m t b", t=PAIR, b=2),
+        )
+        nc.vector.tensor_copy(
+            out=scales[:].rearrange("p (t m) -> p m t", t=PAIR),
+            in_=scales_raw[:].rearrange("p (m t) -> p m t", t=PAIR),
+        )
         quantize(0)
+        interleave(1)
         quantize(1)
 
-        def unit(g, t, h):
+        def product(g, t, h):
             rows = slice(ROWS * g, ROWS * (g + 1))
             nc.tensor.matmul_mx(
                 out=banks[g][t][:],
@@ -100,18 +93,22 @@ def tile_rows_glin_silu_res_kernel(tc, x, w_words, w_scales, r, out):
                 start=True,
                 stop=True,
             )
-            act = acts.tile([P, HALF], F32)
-            nc.scalar.activation(out=act[:], in_=banks[g][t][:], func=SILU)
             cols = slice(t * N + h * HALF, t * N + (h + 1) * HALF)
-            nc.vector.tensor_tensor(out=res[g][:, cols], in0=act[:], in1=res[g][:, cols], op=ADD)
+            nc.scalar.activation(out=act[g][:, cols], in_=banks[g][t][:], func=SILU)
 
-        unit(0, 0, 0)
-        unit(0, 1, 0)
+        def finish(g):
+            for h in range(2):
+                a = act[g][:].rearrange("p (t n) -> p t n", t=PAIR)[:, :, h * HALF : (h + 1) * HALF]
+                b = res[g][:].rearrange("p (t n) -> p t n", t=PAIR)[:, :, h * HALF : (h + 1) * HALF]
+                nc.vector.tensor_tensor(out=b, in0=a, in1=b, op=ADD)
+            nc.sync.dma_start(out=out[g].rearrange("(p t) n -> p (t n)", t=PAIR), in_=res[g][:])
+
+        for t in range(PAIR):
+            product(0, t, 0)
         for g in range(G):
             if g + 1 < G:
-                unit(g + 1, 0, 0)
-            unit(g, 0, 1)
-            unit(g, 1, 1)
-            nc.sync.dma_start(out=out[g].rearrange("(p t) n -> p (t n)", t=PAIR), in_=res[g][:])
-            if g + 1 < G:
-                unit(g + 1, 1, 0)
+                for t in range(PAIR):
+                    product(g + 1, t, 0)
+            for t in range(PAIR):
+                product(g, t, 1)
+            finish(g)

@@ -21,7 +21,6 @@ ROWS = D // PACK
 BLOCKS = D // 32
 PAIR = M // P
 HALF = 512
-RUN = 4
 
 
 def tile_rows_glin_silu_res_kernel(tc, x, w_words, w_scales, r, out):
@@ -31,7 +30,7 @@ def tile_rows_glin_silu_res_kernel(tc, x, w_words, w_scales, r, out):
         psum = ctx.enter_context(tc.psum_pool(name="psum", bufs=1))
         ctx.enter_context(tc.manual_schedule())
 
-        x_raw = [keep.tile([P, PACK, HALF], F32, name="x_raw%d" % h) for h in range(2)]
+        x_raw = [keep.tile([P, 2, N], F32, name="x_raw%d" % u) for u in range(2)]
         words_raw = keep.tile([P, 2 * M], U8, align_bytes=64)
         scales_raw = keep.tile([P, M], U8, align_bytes=64)
         words = keep.tile([P, 2 * M], U8, align_bytes=64)
@@ -46,20 +45,20 @@ def tile_rows_glin_silu_res_kernel(tc, x, w_words, w_scales, r, out):
         nc.vector.memset(scales_raw[:].bitcast(I32), 0)
 
         x_rows = x.rearrange("g (p j) n -> (g p) j n", j=PACK)
-        nc.sync.dma_start(out=x_raw[0][:], in_=x_rows[:, :, 0:HALF])
+        nc.sync.dma_start(out=x_raw[0][:], in_=x_rows[:, 0:2, :])
         nc.sync.dma_start(out=words_raw[:].bitcast(I32), in_=w_words.rearrange("g p b -> (g p) b").bitcast(I32))
         for g in range(G):
             nc.sync.dma_start(
                 out=scales_raw[ROWS * g : ROWS * g + BLOCKS, :].bitcast(I32), in_=w_scales[g].bitcast(I32)
             )
-        nc.sync.dma_start(out=x_raw[1][:], in_=x_rows[:, :, HALF:N])
+        nc.sync.dma_start(out=x_raw[1][:], in_=x_rows[:, 2:4, :])
         for g in range(G):
             nc.sync.dma_start(out=res[g][:], in_=r[g].rearrange("(p t) n -> p (t n)", t=PAIR))
 
-        def interleave(h):
-            nc.vector.tensor_copy(
-                out=grouped[h][:].rearrange("p (c i) j -> p c j i", i=RUN),
-                in_=x_raw[h][:].rearrange("p j (c i) -> p c j i", i=RUN),
+        def views(u, h):
+            return (
+                grouped[h][:, :, 2 * u : 2 * u + 2],
+                x_raw[u][:, :, h * HALF : (h + 1) * HALF].rearrange("p e c -> p c e"),
             )
 
         def quantize(h):
@@ -69,7 +68,10 @@ def tile_rows_glin_silu_res_kernel(tc, x, w_words, w_scales, r, out):
                 in_=grouped[h][:].rearrange("p c j -> p (c j)"),
             )
 
-        interleave(0)
+        dst, src = views(0, 0)
+        nc.vector.tensor_copy(out=dst, in_=src)
+        dst, src = views(0, 1)
+        nc.scalar.copy(out=dst, in_=src)
         nc.vector.tensor_copy(
             out=words[:].rearrange("p (t m b) -> p m t b", t=PAIR, b=2),
             in_=words_raw[:].rearrange("p (m t b) -> p m t b", t=PAIR, b=2),
@@ -78,9 +80,10 @@ def tile_rows_glin_silu_res_kernel(tc, x, w_words, w_scales, r, out):
             out=scales[:].rearrange("p (t m) -> p m t", t=PAIR),
             in_=scales_raw[:].rearrange("p (m t) -> p m t", t=PAIR),
         )
-        quantize(0)
-        interleave(1)
-        quantize(1)
+        for h in range(2):
+            dst, src = views(1, h)
+            nc.vector.tensor_copy(out=dst, in_=src)
+            quantize(h)
 
         def product(g, t, h):
             rows = slice(ROWS * g, ROWS * (g + 1))
@@ -96,19 +99,26 @@ def tile_rows_glin_silu_res_kernel(tc, x, w_words, w_scales, r, out):
             cols = slice(t * N + h * HALF, t * N + (h + 1) * HALF)
             nc.scalar.activation(out=act[g][:, cols], in_=banks[g][t][:], func=SILU)
 
-        def finish(g):
-            for h in range(2):
-                a = act[g][:].rearrange("p (t n) -> p t n", t=PAIR)[:, :, h * HALF : (h + 1) * HALF]
-                b = res[g][:].rearrange("p (t n) -> p t n", t=PAIR)[:, :, h * HALF : (h + 1) * HALF]
-                nc.vector.tensor_tensor(out=b, in0=a, in1=b, op=ADD)
-            nc.sync.dma_start(out=out[g].rearrange("(p t) n -> p (t n)", t=PAIR), in_=res[g][:])
+        def add_residual(g, t, h):
+            cols = slice(t * N + h * HALF, t * N + (h + 1) * HALF)
+            nc.vector.tensor_tensor(out=res[g][:, cols], in0=act[g][:, cols], in1=res[g][:, cols], op=ADD)
 
-        for t in range(PAIR):
-            product(0, t, 0)
+        def finish(g):
+            out_rows = out[g].rearrange("(p t) n -> p (t n)", t=PAIR)
+            first = [tile[:].rearrange("p (t n) -> p t n", t=PAIR)[:, :, 0:HALF] for tile in (act[g], res[g])]
+            nc.vector.tensor_tensor(out=first[1], in0=first[0], in1=first[1], op=ADD)
+            for t in range(PAIR):
+                add_residual(g, t, 1)
+                if g == G - 1:
+                    nc.sync.dma_start(out=out_rows[:, t * N : (t + 1) * N], in_=res[g][:, t * N : (t + 1) * N])
+            if g < G - 1:
+                nc.sync.dma_start(out=out_rows, in_=res[g][:])
+
+        product(0, 0, 0)
         for g in range(G):
+            product(g, 1, 0)
             if g + 1 < G:
-                for t in range(PAIR):
-                    product(g + 1, t, 0)
+                product(g + 1, 0, 0)
             for t in range(PAIR):
                 product(g, t, 1)
             finish(g)

@@ -21,6 +21,7 @@ ROWS = D // PACK
 BLOCKS = D // 32
 PAIR = M // P
 HALF = 512
+QUARTER = 256
 
 
 def tile_rows_glin_silu_res_kernel(tc, x, w_words, w_scales, r, out):
@@ -37,7 +38,7 @@ def tile_rows_glin_silu_res_kernel(tc, x, w_words, w_scales, r, out):
         scales = keep.tile([P, M], U8, align_bytes=64)
         act = [keep.tile([P, PAIR * N], F32, name="act%d" % g) for g in range(G)]
         res = [keep.tile([P, PAIR * N], F32, name="res%d" % g) for g in range(G)]
-        grouped = [keep.tile([P, HALF, PACK], BF16, name="grouped%d" % h, align_bytes=64) for h in range(2)]
+        grouped = [keep.tile([P, QUARTER, PACK], BF16, name="grouped%d" % q, align_bytes=64) for q in range(4)]
         codes = [keep.tile([P, HALF], U32, name="codes%d" % h, align_bytes=64) for h in range(2)]
         planes = [keep.tile([P, HALF], U8, name="planes%d" % h, align_bytes=64) for h in range(2)]
         banks = [[psum.tile([P, HALF], F32, name="bank%d_%d" % (g, t)) for t in range(PAIR)] for g in range(G)]
@@ -46,32 +47,34 @@ def tile_rows_glin_silu_res_kernel(tc, x, w_words, w_scales, r, out):
 
         x_rows = x.rearrange("g (p j) n -> (g p) j n", j=PACK)
         nc.sync.dma_start(out=x_raw[0][:], in_=x_rows[:, 0:2, :])
-        nc.sync.dma_start(out=words_raw[:].bitcast(I32), in_=w_words.rearrange("g p b -> (g p) b").bitcast(I32))
+        nc.scalar.dma_start(out=words_raw[:].bitcast(I32), in_=w_words.rearrange("g p b -> (g p) b").bitcast(I32))
         for g in range(G):
-            nc.sync.dma_start(
+            nc.scalar.dma_start(
                 out=scales_raw[ROWS * g : ROWS * g + BLOCKS, :].bitcast(I32), in_=w_scales[g].bitcast(I32)
             )
         nc.sync.dma_start(out=x_raw[1][:], in_=x_rows[:, 2:4, :])
         for g in range(G):
             nc.sync.dma_start(out=res[g][:], in_=r[g].rearrange("(p t) n -> p (t n)", t=PAIR))
 
-        def views(u, h):
+        def views(u, q):
             return (
-                grouped[h][:, :, 2 * u : 2 * u + 2],
-                x_raw[u][:, :, h * HALF : (h + 1) * HALF].rearrange("p e c -> p c e"),
+                grouped[q][:, :, 2 * u : 2 * u + 2],
+                x_raw[u][:, :, q * QUARTER : (q + 1) * QUARTER].rearrange("p e c -> p c e"),
             )
 
-        def quantize(h):
+        def quantize(q):
+            cols = slice((q % 2) * QUARTER, (q % 2 + 1) * QUARTER)
             nc.vector.quantize_mx(
-                out=codes[h][:].bitcast(FP8X4),
-                scales=planes[h][:],
-                in_=grouped[h][:].rearrange("p c j -> p (c j)"),
+                out=codes[q // 2][:, cols].bitcast(FP8X4),
+                scales=planes[q // 2][:, cols],
+                in_=grouped[q][:].rearrange("p c j -> p (c j)"),
             )
 
-        dst, src = views(0, 0)
-        nc.vector.tensor_copy(out=dst, in_=src)
-        dst, src = views(0, 1)
-        nc.scalar.copy(out=dst, in_=src)
+        for q in range(2):
+            dst, src = views(0, q)
+            nc.vector.tensor_copy(out=dst, in_=src)
+            dst, src = views(0, q + 2)
+            nc.scalar.copy(out=dst, in_=src)
         nc.vector.tensor_copy(
             out=words[:].rearrange("p (t m b) -> p m t b", t=PAIR, b=2),
             in_=words_raw[:].rearrange("p (m t b) -> p m t b", t=PAIR, b=2),
@@ -81,9 +84,11 @@ def tile_rows_glin_silu_res_kernel(tc, x, w_words, w_scales, r, out):
             in_=scales_raw[:].rearrange("p (m t) -> p m t", t=PAIR),
         )
         for h in range(2):
-            dst, src = views(1, h)
-            nc.vector.tensor_copy(out=dst, in_=src)
-            quantize(h)
+            for q in (2 * h, 2 * h + 1):
+                dst, src = views(1, q)
+                nc.vector.tensor_copy(out=dst, in_=src)
+            for q in (2 * h, 2 * h + 1):
+                quantize(q)
 
         def product(g, t, h):
             rows = slice(ROWS * g, ROWS * (g + 1))
@@ -109,10 +114,7 @@ def tile_rows_glin_silu_res_kernel(tc, x, w_words, w_scales, r, out):
             nc.vector.tensor_tensor(out=first[1], in0=first[0], in1=first[1], op=ADD)
             for t in range(PAIR):
                 add_residual(g, t, 1)
-                if g == G - 1:
-                    nc.sync.dma_start(out=out_rows[:, t * N : (t + 1) * N], in_=res[g][:, t * N : (t + 1) * N])
-            if g < G - 1:
-                nc.sync.dma_start(out=out_rows, in_=res[g][:])
+            nc.sync.dma_start(out=out_rows, in_=res[g][:])
 
         product(0, 0, 0)
         for g in range(G):

@@ -49,17 +49,17 @@ def tile_rows_glin_silu_res_kernel(tc, x, w_words, w_scales, r, out):
         nc.sync.dma_start(out=x_raw[0][:], in_=x_rows[:, 0:2, :])
         nc.scalar.dma_start(out=words_raw[:].bitcast(I32), in_=w_words.rearrange("g p b -> (g p) b").bitcast(I32))
         for g in range(G):
-            nc.scalar.dma_start(
+            nc.sync.dma_start(
                 out=scales_raw[ROWS * g : ROWS * g + BLOCKS, :].bitcast(I32), in_=w_scales[g].bitcast(I32)
             )
         nc.sync.dma_start(out=x_raw[1][:], in_=x_rows[:, 2:4, :])
         for g in range(G):
             nc.sync.dma_start(out=res[g][:], in_=r[g].rearrange("(p t) n -> p (t n)", t=PAIR))
 
-        def views(u, q):
+        def views(u, q, first=0, last=QUARTER):
             return (
-                grouped[q][:, :, 2 * u : 2 * u + 2],
-                x_raw[u][:, :, q * QUARTER : (q + 1) * QUARTER].rearrange("p e c -> p c e"),
+                grouped[q][:, first:last, 2 * u : 2 * u + 2],
+                x_raw[u][:, :, q * QUARTER + first : q * QUARTER + last].rearrange("p e c -> p c e"),
             )
 
         def quantize(q):
@@ -70,23 +70,26 @@ def tile_rows_glin_silu_res_kernel(tc, x, w_words, w_scales, r, out):
                 in_=grouped[q][:].rearrange("p c j -> p (c j)"),
             )
 
+        nc.vector.tensor_copy(
+            out=words[:].rearrange("p (t m b) -> p m t b", t=PAIR, b=2),
+            in_=words_raw[:].rearrange("p (m t b) -> p m t b", t=PAIR, b=2),
+        )
         for q in range(2):
             dst, src = views(0, q)
             nc.vector.tensor_copy(out=dst, in_=src)
             dst, src = views(0, q + 2)
             nc.scalar.copy(out=dst, in_=src)
         nc.vector.tensor_copy(
-            out=words[:].rearrange("p (t m b) -> p m t b", t=PAIR, b=2),
-            in_=words_raw[:].rearrange("p (m t b) -> p m t b", t=PAIR, b=2),
-        )
-        nc.vector.tensor_copy(
             out=scales[:].rearrange("p (t m) -> p m t", t=PAIR),
             in_=scales_raw[:].rearrange("p (m t) -> p m t", t=PAIR),
         )
         for h in range(2):
             for q in (2 * h, 2 * h + 1):
-                dst, src = views(1, q)
+                dst, src = views(1, q, 0, QUARTER // 2 if q == 1 else QUARTER)
                 nc.vector.tensor_copy(out=dst, in_=src)
+            if h == 0:
+                dst, src = views(1, 1, QUARTER // 2, QUARTER)
+                nc.scalar.copy(out=dst, in_=src)
             for q in (2 * h, 2 * h + 1):
                 quantize(q)
 

@@ -22,6 +22,7 @@ BLOCKS = D // 32
 PAIR = M // P
 HALF = 512
 QUARTER = 256
+LINE = 4
 
 
 def tile_rows_glin_silu_res_kernel(tc, x, w_words, w_scales, r, out):
@@ -31,8 +32,9 @@ def tile_rows_glin_silu_res_kernel(tc, x, w_words, w_scales, r, out):
         psum = ctx.enter_context(tc.psum_pool(name="psum", bufs=1))
         ctx.enter_context(tc.manual_schedule())
 
-        x_raw = [keep.tile([P, 2, N], F32, name="x_raw%d" % u) for u in range(2)]
+        x_raw = keep.tile([P, PACK, N], F32)
         words_raw = keep.tile([P, 2 * M], U8, align_bytes=64)
+        scales_in = keep.tile([P, M], U8, align_bytes=64)
         scales_raw = keep.tile([P, M], U8, align_bytes=64)
         words = keep.tile([P, 2 * M], U8, align_bytes=64)
         scales = keep.tile([P, M], U8, align_bytes=64)
@@ -43,23 +45,32 @@ def tile_rows_glin_silu_res_kernel(tc, x, w_words, w_scales, r, out):
         planes = [keep.tile([P, HALF], U8, name="planes%d" % h, align_bytes=64) for h in range(2)]
         banks = [[psum.tile([P, HALF], F32, name="bank%d_%d" % (g, t)) for t in range(PAIR)] for g in range(G)]
 
-        nc.vector.memset(scales_raw[:].bitcast(I32), 0)
-
-        x_rows = x.rearrange("g (p j) n -> (g p) j n", j=PACK)
-        nc.sync.dma_start(out=x_raw[0][:], in_=x_rows[:, 0:2, :])
-        nc.scalar.dma_start(out=words_raw[:].bitcast(I32), in_=w_words.rearrange("g p b -> (g p) b").bitcast(I32))
+        scale_rows = [slice(ROWS * g, ROWS * g + BLOCKS) for g in range(G)]
+        nc.sync.dma_start(out=words_raw[:].bitcast(I32), in_=w_words.rearrange("g p b -> (g p) b").bitcast(I32))
         for g in range(G):
-            nc.sync.dma_start(
-                out=scales_raw[ROWS * g : ROWS * g + BLOCKS, :].bitcast(I32), in_=w_scales[g].bitcast(I32)
-            )
-        nc.sync.dma_start(out=x_raw[1][:], in_=x_rows[:, 2:4, :])
+            nc.scalar.dma_start(out=scales_in[scale_rows[g], :].bitcast(I32), in_=w_scales[g].bitcast(I32))
+        nc.sync.dma_start(out=x_raw[:], in_=x.rearrange("g (p j) n -> (g p) j n", j=PACK))
         for g in range(G):
             nc.sync.dma_start(out=res[g][:], in_=r[g].rearrange("(p t) n -> p (t n)", t=PAIR))
 
-        def views(u, q, first=0, last=QUARTER):
-            return (
-                grouped[q][:, first:last, 2 * u : 2 * u + 2],
-                x_raw[u][:, :, q * QUARTER + first : q * QUARTER + last].rearrange("p e c -> p c e"),
+        nc.vector.memset(scales_raw[:].bitcast(I32), 0)
+        nc.vector.tensor_copy(
+            out=words[:].rearrange("p (t m b) -> p m t b", t=PAIR, b=2),
+            in_=words_raw[:].rearrange("p (m t b) -> p m t b", t=PAIR, b=2),
+        )
+        for g in range(G):
+            nc.vector.tensor_copy(
+                out=scales_raw[scale_rows[g], :].bitcast(I32), in_=scales_in[scale_rows[g], :].bitcast(I32)
+            )
+        nc.vector.tensor_copy(
+            out=scales[:].rearrange("p (t m) -> p m t", t=PAIR),
+            in_=scales_raw[:].rearrange("p (m t) -> p m t", t=PAIR),
+        )
+
+        def interleave(q):
+            nc.vector.tensor_copy(
+                out=grouped[q][:].rearrange("p (c i) j -> p c j i", i=LINE),
+                in_=x_raw[:, :, q * QUARTER : (q + 1) * QUARTER].rearrange("p j (c i) -> p c j i", i=LINE),
             )
 
         def quantize(q):
@@ -70,26 +81,9 @@ def tile_rows_glin_silu_res_kernel(tc, x, w_words, w_scales, r, out):
                 in_=grouped[q][:].rearrange("p c j -> p (c j)"),
             )
 
-        nc.vector.tensor_copy(
-            out=words[:].rearrange("p (t m b) -> p m t b", t=PAIR, b=2),
-            in_=words_raw[:].rearrange("p (m t b) -> p m t b", t=PAIR, b=2),
-        )
-        for q in range(2):
-            dst, src = views(0, q)
-            nc.vector.tensor_copy(out=dst, in_=src)
-            dst, src = views(0, q + 2)
-            nc.scalar.copy(out=dst, in_=src)
-        nc.vector.tensor_copy(
-            out=scales[:].rearrange("p (t m) -> p m t", t=PAIR),
-            in_=scales_raw[:].rearrange("p (m t) -> p m t", t=PAIR),
-        )
         for h in range(2):
             for q in (2 * h, 2 * h + 1):
-                dst, src = views(1, q, 0, QUARTER // 2 if q == 1 else QUARTER)
-                nc.vector.tensor_copy(out=dst, in_=src)
-            if h == 0:
-                dst, src = views(1, 1, QUARTER // 2, QUARTER)
-                nc.scalar.copy(out=dst, in_=src)
+                interleave(q)
             for q in (2 * h, 2 * h + 1):
                 quantize(q)
 

@@ -22,7 +22,7 @@ BLOCKS = D // 32
 PAIR = M // P
 HALF = 512
 QUARTER = 256
-LINE = 4
+LINE = 2
 
 
 def tile_rows_glin_silu_res_kernel(tc, x, w_words, w_scales, r, out):
@@ -34,7 +34,6 @@ def tile_rows_glin_silu_res_kernel(tc, x, w_words, w_scales, r, out):
 
         x_raw = keep.tile([P, PACK, N], F32)
         words_raw = keep.tile([P, 2 * M], U8, align_bytes=64)
-        scales_in = keep.tile([P, M], U8, align_bytes=64)
         scales_raw = keep.tile([P, M], U8, align_bytes=64)
         words = keep.tile([P, 2 * M], U8, align_bytes=64)
         scales = keep.tile([P, M], U8, align_bytes=64)
@@ -45,32 +44,25 @@ def tile_rows_glin_silu_res_kernel(tc, x, w_words, w_scales, r, out):
         planes = [keep.tile([P, HALF], U8, name="planes%d" % h, align_bytes=64) for h in range(2)]
         banks = [[psum.tile([P, HALF], F32, name="bank%d_%d" % (g, t)) for t in range(PAIR)] for g in range(G)]
 
-        scale_rows = [slice(ROWS * g, ROWS * g + BLOCKS) for g in range(G)]
+        nc.vector.memset(scales_raw[:].bitcast(I32), 0)
         nc.sync.dma_start(out=words_raw[:].bitcast(I32), in_=w_words.rearrange("g p b -> (g p) b").bitcast(I32))
-        for g in range(G):
-            nc.scalar.dma_start(out=scales_in[scale_rows[g], :].bitcast(I32), in_=w_scales[g].bitcast(I32))
         nc.sync.dma_start(out=x_raw[:], in_=x.rearrange("g (p j) n -> (g p) j n", j=PACK))
+        for g in range(G):
+            nc.sync.dma_start(
+                out=scales_raw[ROWS * g : ROWS * g + BLOCKS, :].bitcast(I32), in_=w_scales[g].bitcast(I32)
+            )
         for g in range(G):
             nc.sync.dma_start(out=res[g][:], in_=r[g].rearrange("(p t) n -> p (t n)", t=PAIR))
 
-        nc.vector.memset(scales_raw[:].bitcast(I32), 0)
         nc.vector.tensor_copy(
             out=words[:].rearrange("p (t m b) -> p m t b", t=PAIR, b=2),
             in_=words_raw[:].rearrange("p (m t b) -> p m t b", t=PAIR, b=2),
         )
-        for g in range(G):
-            nc.vector.tensor_copy(
-                out=scales_raw[scale_rows[g], :].bitcast(I32), in_=scales_in[scale_rows[g], :].bitcast(I32)
-            )
-        nc.vector.tensor_copy(
-            out=scales[:].rearrange("p (t m) -> p m t", t=PAIR),
-            in_=scales_raw[:].rearrange("p (m t) -> p m t", t=PAIR),
-        )
 
-        def interleave(q):
-            nc.vector.tensor_copy(
-                out=grouped[q][:].rearrange("p (c i) j -> p c j i", i=LINE),
-                in_=x_raw[:, :, q * QUARTER : (q + 1) * QUARTER].rearrange("p j (c i) -> p c j i", i=LINE),
+        def views(q, first=0, last=QUARTER):
+            return (
+                grouped[q][:, first:last, :].rearrange("p (c i) j -> p c j i", i=LINE),
+                x_raw[:, :, q * QUARTER + first : q * QUARTER + last].rearrange("p j (c i) -> p c j i", i=LINE),
             )
 
         def quantize(q):
@@ -81,11 +73,22 @@ def tile_rows_glin_silu_res_kernel(tc, x, w_words, w_scales, r, out):
                 in_=grouped[q][:].rearrange("p c j -> p (c j)"),
             )
 
-        for h in range(2):
-            for q in (2 * h, 2 * h + 1):
-                interleave(q)
-            for q in (2 * h, 2 * h + 1):
-                quantize(q)
+        dst, src = views(1, QUARTER // 2, QUARTER)
+        nc.scalar.copy(out=dst, in_=src)
+        for q in (0, 1):
+            dst, src = views(q, 0, QUARTER // 2 if q == 1 else QUARTER)
+            nc.vector.tensor_copy(out=dst, in_=src)
+        quantize(0)
+        nc.vector.tensor_copy(
+            out=scales[:].rearrange("p (t m) -> p m t", t=PAIR),
+            in_=scales_raw[:].rearrange("p (m t) -> p m t", t=PAIR),
+        )
+        quantize(1)
+        for q in (2, 3):
+            dst, src = views(q)
+            nc.vector.tensor_copy(out=dst, in_=src)
+        for q in (2, 3):
+            quantize(q)
 
         def product(g, t, h):
             rows = slice(ROWS * g, ROWS * (g + 1))

@@ -45,7 +45,7 @@ def tile_rows_glin_silu_res_kernel(tc, x, w_words, w_scales, r, out):
         banks = [[psum.tile([P, HALF], F32, name="bank%d_%d" % (g, t)) for t in range(PAIR)] for g in range(G)]
 
         nc.vector.memset(scales_raw[:].bitcast(I32), 0)
-        nc.sync.dma_start(out=words_raw[:].bitcast(I32), in_=w_words.rearrange("g p b -> (g p) b").bitcast(I32))
+        nc.scalar.dma_start(out=words_raw[:].bitcast(I32), in_=w_words.rearrange("g p b -> (g p) b").bitcast(I32))
         nc.sync.dma_start(out=x_raw[:], in_=x.rearrange("g (p j) n -> (g p) j n", j=PACK))
         for g in range(G):
             nc.sync.dma_start(

@@ -47,9 +47,11 @@ def tile_rows_glin_silu_res_kernel(tc, x, w_words, w_scales, r, out):
         nc.vector.memset(scales_raw[:].bitcast(I32), 0)
         nc.scalar.dma_start(out=words_raw[:].bitcast(I32), in_=w_words.rearrange("g p b -> (g p) b").bitcast(I32))
         nc.sync.dma_start(out=x_raw[:], in_=x.rearrange("g (p j) n -> (g p) j n", j=PACK))
-        for g in range(G):
+        pieces = [(g, 0, BLOCKS) for g in range(G - 1)] + [(G - 1, 0, BLOCKS // 2), (G - 1, BLOCKS // 2, BLOCKS)]
+        for g, first, last in pieces:
             nc.sync.dma_start(
-                out=scales_raw[ROWS * g : ROWS * g + BLOCKS, :].bitcast(I32), in_=w_scales[g].bitcast(I32)
+                out=scales_raw[ROWS * g + first : ROWS * g + last, :].bitcast(I32),
+                in_=w_scales[g, first:last, :].bitcast(I32),
             )
         for g in range(G):
             nc.sync.dma_start(out=res[g][:], in_=r[g].rearrange("(p t) n -> p (t n)", t=PAIR))

from contextlib import ExitStack

import concourse.mybir as mybir

G, D, M, N = 4, 128, 256, 1024
FLOPS = 2 * G * D * M * N

F32 = mybir.dt.float32
BF16 = mybir.dt.bfloat16
I32 = mybir.dt.int32
U32 = mybir.dt.uint32
U8 = mybir.dt.uint8
FP8X4 = mybir.dt.float8_e4m3fn_x4
FP4X4 = mybir.dt.float4_e2m1fn_x4
SILU = mybir.ActivationFunctionType.Silu
ADD = mybir.AluOpType.add

P = 128
PACK = 4
ROWS = D // PACK
BLOCKS = D // 32
PAIR = M // P
HALF = 512
QUARTER = 256
LINE = 2


def tile_rows_glin_silu_res_kernel(tc, x, w_words, w_scales, r, out):
    nc = tc.nc
    with ExitStack() as ctx:
        keep = ctx.enter_context(tc.tile_pool(name="keep", bufs=1))
        psum = ctx.enter_context(tc.psum_pool(name="psum", bufs=1))
        ctx.enter_context(tc.manual_schedule())

        x_raw = keep.tile([P, PACK, N], F32)
        words_raw = keep.tile([P, 2 * M], U8, align_bytes=64)
        scales_raw = keep.tile([P, M], U8, align_bytes=64)
        words = keep.tile([P, 2 * M], U8, align_bytes=64)
        scales = keep.tile([P, M], U8, align_bytes=64)
        act = [keep.tile([P, PAIR * N], F32, name="act%d" % g) for g in range(G)]
        res = [keep.tile([P, PAIR * N], F32, name="res%d" % g) for g in range(G)]
        grouped = [keep.tile([P, QUARTER, PACK], BF16, name="grouped%d" % q, align_bytes=64) for q in range(4)]
        codes = [keep.tile([P, HALF], U32, name="codes%d" % h, align_bytes=64) for h in range(2)]
        planes = [keep.tile([P, HALF], U8, name="planes%d" % h, align_bytes=64) for h in range(2)]
        banks = [[psum.tile([P, HALF], F32, name="bank%d_%d" % (g, t)) for t in range(PAIR)] for g in range(G)]

        nc.vector.memset(scales_raw[:].bitcast(I32), 0)
        nc.scalar.dma_start(out=words_raw[:].bitcast(I32), in_=w_words.rearrange("g p b -> (g p) b").bitcast(I32))
        nc.sync.dma_start(out=x_raw[:], in_=x.rearrange("g (p j) n -> (g p) j n", j=PACK))
        pieces = [(g, 0, BLOCKS) for g in range(G - 1)] + [(G - 1, 0, BLOCKS // 2), (G - 1, BLOCKS // 2, BLOCKS)]
        for g, first, last in pieces:
            nc.sync.dma_start(
                out=scales_raw[ROWS * g + first : ROWS * g + last, :].bitcast(I32),
                in_=w_scales[g, first:last, :].bitcast(I32),
            )
        for g in range(G):
            nc.sync.dma_start(out=res[g][:], in_=r[g].rearrange("(p t) n -> p (t n)", t=PAIR))

        nc.vector.tensor_copy(
            out=words[:].rearrange("p (t m b) -> p m t b", t=PAIR, b=2),
            in_=words_raw[:].rearrange("p (m t b) -> p m t b", t=PAIR, b=2),
        )

        def views(q, first=0, last=QUARTER):
            return (
                grouped[q][:, first:last, :].rearrange("p (c i) j -> p c j i", i=LINE),
                x_raw[:, :, q * QUARTER + first : q * QUARTER + last].rearrange("p j (c i) -> p c j i", i=LINE),
            )

        def quantize(q):
            cols = slice((q % 2) * QUARTER, (q % 2 + 1) * QUARTER)
            nc.vector.quantize_mx(
                out=codes[q // 2][:, cols].bitcast(FP8X4),
                scales=planes[q // 2][:, cols],
                in_=grouped[q][:].rearrange("p c j -> p (c j)"),
            )

        dst, src = views(1, QUARTER // 2, QUARTER)
        nc.scalar.copy(out=dst, in_=src)
        for q in (0, 1):
            dst, src = views(q, 0, QUARTER // 2 if q == 1 else QUARTER)
            nc.vector.tensor_copy(out=dst, in_=src)
        quantize(0)
        nc.vector.tensor_copy(
            out=scales[:].rearrange("p (t m) -> p m t", t=PAIR),
            in_=scales_raw[:].rearrange("p (m t) -> p m t", t=PAIR),
        )
        quantize(1)
        for q in (2, 3):
            dst, src = views(q)
            nc.vector.tensor_copy(out=dst, in_=src)
        for q in (2, 3):
            quantize(q)

        def product(g, t, h):
            rows = slice(ROWS * g, ROWS * (g + 1))
            nc.tensor.matmul_mx(
                out=banks[g][t][:],
                lhsT=words[rows, 2 * P * t : 2 * P * (t + 1)].bitcast(FP4X4),
                lhsT_scale=scales[rows, P * t : P * (t + 1)],
                rhs=codes[h][rows, :].bitcast(FP8X4),
                rhs_scale=planes[h][rows, :],
                start=True,
                stop=True,
            )
            cols = slice(t * N + h * HALF, t * N + (h + 1) * HALF)
            nc.scalar.activation(out=act[g][:, cols], in_=banks[g][t][:], func=SILU)

        def add_residual(g, t, h):
            cols = slice(t * N + h * HALF, t * N + (h + 1) * HALF)
            nc.vector.tensor_tensor(out=res[g][:, cols], in0=act[g][:, cols], in1=res[g][:, cols], op=ADD)

        def finish(g):
            out_rows = out[g].rearrange("(p t) n -> p (t n)", t=PAIR)
            first = [tile[:].rearrange("p (t n) -> p t n", t=PAIR)[:, :, 0:HALF] for tile in (act[g], res[g])]
            nc.vector.tensor_tensor(out=first[1], in0=first[0], in1=first[1], op=ADD)
            for t in range(PAIR):
                add_residual(g, t, 1)
            nc.sync.dma_start(out=out_rows, in_=res[g][:])

        product(0, 0, 0)
        for g in range(G):
            product(g, 1, 0)
            if g + 1 < G:
                product(g + 1, 0, 0)
            for t in range(PAIR):
                product(g, t, 1)
            finish(g)
